import numpy as np
import ml_dtypes


def mxq(x, axis, fmt="e4m3"):
    dtype, down = {"e4m3": (ml_dtypes.float8_e4m3fn, 7), "e5m2": (ml_dtypes.float8_e5m2, 14)}[fmt]
    v = np.moveaxis(np.asarray(x, np.float32).astype(ml_dtypes.bfloat16).astype(np.float64), axis, -1)
    blocks = v.reshape(v.shape[:-1] + (-1, 32))
    amax = np.abs(blocks).max(-1, keepdims=True)
    byte = np.maximum(np.where(amax > 0, np.frexp(amax)[1] - 1 + 127, 0) - down, 1)
    scale = np.exp2(byte - 127.0)
    codes = (blocks / scale).astype(np.float32).astype(dtype).astype(np.float64)
    return np.moveaxis((codes * scale).reshape(v.shape), -1, axis)


WIDE = False


def mx_kscale(k):
    if not WIDE:
        return np.ones(k)
    levels = np.array([10, -10, 5, -5, 0])
    if k % 512:
        return np.exp2(np.random.permutation(np.resize(levels, k // 32))).repeat(32)
    a = np.empty((k // 512, 16))
    for p in range(k // 512):
        a[p, :8] = np.random.permutation(np.resize(levels, 8))
        for g in range(8):
            far = levels[np.abs(levels - a[p, g]) >= 10]
            a[p, g + 8] = far[np.random.randint(len(far))]
    return np.exp2(a.ravel()).repeat(32)


BF16 = ml_dtypes.bfloat16


def bf(x):
    return np.asarray(x, np.float32).astype(BF16)


def f64(x):
    return np.asarray(x).astype(np.float64)


N, C, J = 2048, 1024, 1024
SHRINK_LO, SHRINK_HI = 0.6, 1.0
SIGMA_SPREAD = 0.3
CUTOFF = 0.1


def setup_inputs():
    s, t = mx_kscale(N), mx_kscale(C)
    x = np.random.standard_normal((N, C)) / np.sqrt(C)
    p = np.linalg.pinv(x, CUTOFF)
    return {"pinv": bf(p * s * t[:, None]),
            "treat": bf(np.random.standard_normal((N, J)) / s[:, None]),
            "controls": bf(x / s[:, None] / t),
            "shrink": bf(np.random.uniform(SHRINK_LO, SHRINK_HI, C)),
            "sigma": bf(np.exp(SIGMA_SPREAD * np.random.standard_normal(N)) * s)}


def reference(pinv, treat, controls, shrink, sigma):
    d = f64(treat)
    coef = mxq(f64(pinv), 1, "e4m3") @ mxq(d, 0, "e4m3")
    coef = coef * f64(shrink)[:, None]
    fit = mxq(f64(controls), 1, "e4m3") @ mxq(coef, 0, "e4m3")
    return (d - fit) * f64(sigma)[:, None]

@@ -1,0 +1,286 @@
+from contextlib import ExitStack
+
+import concourse.mybir as mybir
+from concourse.masks import make_identity
+
+N_OBS, N_CTRL, N_TREAT = 2048, 1024, 1024
+FLOPS = 2 * N_CTRL * N_OBS * N_TREAT + 2 * N_OBS * N_CTRL * N_TREAT
+
+F32 = mybir.dt.float32
+BF16 = mybir.dt.bfloat16
+U32 = mybir.dt.uint32
+U8 = mybir.dt.uint8
+FP8X4 = mybir.dt.float8_e4m3fn_x4
+COPY = mybir.ActivationFunctionType.Copy
+MULT = mybir.AluOpType.mult
+SUBTRACT = mybir.AluOpType.subtract
+
+P = 128
+PACK = 4
+K_PASS = P * PACK
+HALF = 512
+UNIT = 2048
+OBS_PASSES = N_OBS // K_PASS
+CTRL_PASSES = N_CTRL // K_PASS
+V_COLS = 384
+RUN = 4
+
+
+def tile_shrunken_control_residuals_s7_kernel(tc, pinv, treat, controls, shrink, sigma, out):
+    nc = tc.nc
+    with ExitStack() as ctx:
+        keep = ctx.enter_context(tc.tile_pool(name="keep", bufs=1))
+        ring = ctx.enter_context(tc.tile_pool(name="ring", bufs=2))
+        psum = ctx.enter_context(tc.psum_pool(name="psum", bufs=1))
+        ctx.enter_context(tc.manual_schedule())
+
+        def bank(i):
+            return psum.tile([P, HALF], F32, name="bank%d" % i)
+
+        pinv_raw = [keep.tile([P, UNIT], BF16, name="pinv_raw%d" % s) for s in range(2 * PACK)]
+        treat_raw = [keep.tile([P, 2 * UNIT], BF16, name="treat_raw%d" % k) for k in range(OBS_PASSES)]
+        ctrl_raw = [keep.tile([P, 2 * UNIT], BF16, name="ctrl_raw%d" % g) for g in range(OBS_PASSES)]
+        shrink_bf = keep.tile([P, CTRL_PASSES, PACK], BF16, name="shrink_bf")
+        shrink_f = keep.tile([P, CTRL_PASSES * PACK], F32, name="shrink_f")
+        sigma_bf = keep.tile([P, OBS_PASSES, PACK], BF16, name="sigma_bf")
+        neg_sigma = keep.tile([P, OBS_PASSES * PACK], F32, name="neg_sigma")
+        ident = keep.tile([P, P], F32, name="ident")
+
+        def load_treat(k, h):
+            nc.sync.dma_start(
+                out=treat_raw[k][:, h * UNIT:(h + 1) * UNIT].rearrange("p (t j) -> p t j", t=PACK),
+                in_=treat[k * K_PASS:(k + 1) * K_PASS, h * HALF:(h + 1) * HALF].rearrange("(p t) j -> p t j", t=PACK),
+            )
+
+        nc.scalar.dma_start(out=shrink_bf[:], in_=shrink.rearrange("(g p t) -> p g t", p=P, t=PACK))
+        for k in range(OBS_PASSES):
+            nc.sync.dma_start(
+                out=pinv_raw[k][:].rearrange("p (t k) -> p t k", t=PACK),
+                in_=pinv[0:K_PASS, k * K_PASS:(k + 1) * K_PASS].rearrange("(p t) k -> p t k", t=PACK),
+            )
+            load_treat(k, 0)
+        for t in range(PACK):
+            nc.sync.dma_start(
+                out=pinv_raw[PACK + t][:],
+                in_=pinv[K_PASS:2 * K_PASS, :].rearrange("(p t) k -> p t k", t=PACK)[:, t, :],
+            )
+            load_treat(t, 1)
+        for g in range(OBS_PASSES):
+            rows = controls[g * K_PASS:(g + 1) * K_PASS, :].rearrange("(p t) c -> p (t c)", t=PACK)
+            for u in range(2):
+                nc.sync.dma_start(out=ctrl_raw[g][:, u * UNIT:(u + 1) * UNIT], in_=rows[:, u * UNIT:(u + 1) * UNIT])
+            if g == 0:
+                nc.sync.dma_start(out=sigma_bf[:], in_=sigma.rearrange("(g p t) -> p g t", p=P, t=PACK))
+
+        make_identity(nc, ident[:])
+        nc.scalar.activation(out=shrink_f[:], in_=shrink_bf[:].rearrange("p g t -> p (g t)"), func=COPY)
+
+        mx = {}
+
+        def turn(raw, unit, banks):
+            words = raw[:, unit * UNIT:(unit + 1) * UNIT].bitcast(F32)
+            held = [bank(i) for i in banks]
+            for q in range(4):
+                for u in range(2):
+                    slot = (q % 2) * 2 + u
+                    nc.tensor.transpose(
+                        held[q // 2][:, slot * P:(slot + 1) * P],
+                        words[:, 256 * q + u:256 * (q + 1):2],
+                        ident[:],
+                    )
+            return held
+
+        def unload(held):
+            grouped = ring.tile([P, UNIT], BF16, name="turned", bufs=3, align_bytes=64)
+            words = grouped[:].bitcast(F32)
+            for b in range(2):
+                nc.scalar.copy(
+                    out=words[:, b * HALF:(b + 1) * HALF].rearrange("p (q m u) -> p q m u", q=2, u=2),
+                    in_=held[b][:].rearrange("p (q u m) -> p q m u", q=2, u=2),
+                )
+            return grouped
+
+        def quantise(key, grouped, tag=None, bufs=1):
+            name = tag or "%s_%d_%d" % key
+            codes = keep.tile([P, HALF], U32, name="c_" + name, bufs=bufs, align_bytes=64)
+            scales = keep.tile([P, HALF], U8, name="s_" + name, bufs=bufs, align_bytes=64)
+            nc.vector.quantize_mx(out=codes[:].bitcast(FP8X4), scales=scales[:], in_=grouped[:])
+            mx[key] = (codes, scales)
+
+        def weave(copy, grouped, rows, lo, hi):
+            copy(
+                out=grouped[:, PACK * lo:PACK * hi].rearrange("p (c i t) -> p c t i", i=RUN, t=PACK),
+                in_=rows.rearrange("p (t j) -> p t j", t=PACK)[:, :, lo:hi].rearrange("p t (c i) -> p c t i", i=RUN),
+            )
+
+        def woven():
+            return ring.tile([P, UNIT], BF16, name="woven", bufs=3, align_bytes=64)
+
+        def matmul(acc, left, block, right, start, stop):
+            cols = slice(block * P, (block + 1) * P)
+            nc.tensor.matmul_mx(
+                out=acc[:],
+                lhsT=mx[left][0][:, cols].bitcast(FP8X4),
+                lhsT_scale=mx[left][1][:, cols],
+                rhs=mx[right][0][:].bitcast(FP8X4),
+                rhs_scale=mx[right][1][:],
+                start=start,
+                stop=stop,
+            )
+
+        def coef_pass(acc, h, g, t, k):
+            left, block = (("pinv", 0, k), t) if g == 0 else (("pinv", 1, t), k)
+            matmul(acc, left, block, ("treat", h, k), k == 0, k == OBS_PASSES - 1)
+
+        coef_rows = {}
+
+        def shrink_out(acc, h, g, t, on_vector=False):
+            if (h, g) not in coef_rows:
+                coef_rows[h, g] = ring.tile([P, UNIT], BF16, name="coef_rows", bufs=3)
+            dst = coef_rows[h, g][:, t * HALF:(t + 1) * HALF]
+            factor = shrink_f[:, g * PACK + t:g * PACK + t + 1]
+            if on_vector:
+                nc.vector.tensor_scalar(out=dst, in0=acc[:], scalar1=factor, scalar2=None, op0=MULT)
+            else:
+                nc.scalar.activation(out=dst, in_=acc[:], func=COPY, scale=factor)
+
+        def treat_half(k, h):
+            return treat_raw[k][:, h * UNIT:(h + 1) * UNIT]
+
+        result = {}
+
+        def prescale(g, t, on_vector=False):
+            res = ring.tile([P, N_TREAT], F32, name="result", bufs=9)
+            result[g, t] = res
+            src = treat_raw[g][:].rearrange("p (h t j) -> p h t j", h=2, t=PACK)[:, :, t, :]
+            dst = res[:].rearrange("p (h j) -> p h j", h=2)
+            factor = neg_sigma[:, g * PACK + t:g * PACK + t + 1]
+            if on_vector:
+                nc.vector.tensor_scalar(out=dst, in0=src, scalar1=factor, scalar2=None, op0=MULT)
+            else:
+                nc.scalar.activation(out=dst, in_=src, func=COPY, scale=factor)
+
+        turns = [0]
+
+        def fit(g, t, h):
+            acc = bank(turns[0] % 4)
+            turns[0] = turns[0] + 1
+            for c in range(CTRL_PASSES):
+                matmul(acc, ("ctrl", g, t // 2), (t % 2) * 2 + c, ("coef", h, c), c == 0, c == CTRL_PASSES - 1)
+            return acc
+
+        def finish(acc, g, t, h):
+            part = result[g, t][:, h * HALF:(h + 1) * HALF]
+            nc.vector.scalar_tensor_tensor(
+                out=part, in0=acc[:], scalar=neg_sigma[:, g * PACK + t:g * PACK + t + 1], in1=part,
+                op0=MULT, op1=SUBTRACT,
+            )
+
+        def store(g, t, lo, hi):
+            rows = out[g * K_PASS:(g + 1) * K_PASS, :].rearrange("(p t) j -> p t j", t=PACK)
+            nc.sync.dma_start(out=rows[:, t, lo:hi], in_=result[g, t][:, lo:hi])
+
+        def tile_out(g, t):
+            for h in range(2):
+                finish(fit(g, t, h), g, t, h)
+            store(g, t, 0, N_TREAT)
+
+        def weave_coef(h, g):
+            grouped = woven()
+            weave(nc.vector.tensor_copy, grouped, coef_rows[h, g][:], 0, HALF)
+            return grouped
+
+        def coef_tile(h, g, t):
+            acc = bank(t)
+            for k in range(OBS_PASSES):
+                coef_pass(acc, h, g, t, k)
+            return acc
+
+        def turn_controls(g):
+            return [turn(ctrl_raw[g], u, (4 + 2 * u, 5 + 2 * u)) for u in range(2)]
+
+        accs = [bank(t) for t in range(PACK)]
+        for s in range(2 * PACK):
+            held = turn(pinv_raw[s], 0, (4 + 2 * (s % 2), 5 + 2 * (s % 2)))
+            if 0 < s <= PACK:
+                for t in range(PACK):
+                    coef_pass(accs[t], 0, 0, t, s - 1)
+            elif s > PACK:
+                acc = coef_tile(0, 1, s - PACK - 1)
+            turned = unload(held)
+            grouped = woven()
+            k, h = s % PACK, s // PACK
+            if h == 0:
+                weave(nc.vector.tensor_copy, grouped, treat_half(k, h), 0, V_COLS)
+                weave(nc.scalar.copy, grouped, treat_half(k, h), V_COLS, HALF)
+            else:
+                weave(nc.vector.tensor_copy, grouped, treat_half(k, h), 0, HALF)
+                shrink_out(accs[k], 0, 0, k)
+                if s > PACK:
+                    shrink_out(acc, 0, 1, k - 1)
+            quantise(("pinv", h, k), turned)
+            quantise(("treat", h, k), grouped)
+        held = turn_controls(0)
+        acc = coef_tile(0, 1, PACK - 1)
+        turned = [unload(held[u]) for u in range(2)]
+        shrink_out(acc, 0, 1, PACK - 1)
+        nc.scalar.activation(out=neg_sigma[:], in_=sigma_bf[:].rearrange("p g t -> p (g t)"), func=COPY, scale=-1.0)
+
+        first = weave_coef(0, 0)
+        quantise(("ctrl", 0, 0), turned[0], "ctrl", 4)
+        quantise(("coef", 0, 0), first)
+        second = weave_coef(0, 1)
+        quantise(("ctrl", 0, 1), turned[1], "ctrl", 4)
+        quantise(("coef", 0, 1), second)
+        for t in range(PACK):
+            shrink_out(coef_tile(1, 0, t), 1, 0, t)
+        prescale(0, 0, on_vector=True)
+        first = weave_coef(1, 0)
+        prescale(0, 1, on_vector=True)
+        quantise(("coef", 1, 0), first)
+        prescale(0, 2, on_vector=True)
+        prescale(0, 3, on_vector=True)
+        for t in range(PACK):
+            shrink_out(coef_tile(1, 1, t), 1, 1, t)
+            if t == 0:
+                prescale(1, 0)
+
+        accs = [fit(0, t, 0) for t in range(PACK)]
+        second = weave_coef(1, 1)
+        prescale(1, 1)
+        for t in range(PACK):
+            finish(accs[t], 0, t, 0)
+            store(0, t, 0, HALF)
+            if t == 0:
+                quantise(("coef", 1, 1), second)
+        for g in range(OBS_PASSES):
+            more = g + 1 < OBS_PASSES
+            if g > 0:
+                tile_out(g, 0)
+                tile_out(g, 1)
+            if more:
+                turned = [unload(pair) for pair in turn_controls(g + 1)]
+                quantise(("ctrl", g + 1, 0), turned[0], "ctrl", 4)
+                prescale(g + 1, 2)
+                prescale(g + 1, 3)
+            if g > 0:
+                tile_out(g, 2)
+            else:
+                for t in range(2):
+                    finish(fit(g, t, 1), g, t, 1)
+                    store(g, t, HALF, N_TREAT)
+            if more:
+                quantise(("ctrl", g + 1, 1), turned[1], "ctrl", 4)
+            if g == 0:
+                for t in range(2, 4):
+                    finish(fit(g, t, 1), g, t, 1)
+                    store(g, t, HALF, N_TREAT)
+            elif more:
+                tile_out(g, 3)
+            else:
+                for h in range(2):
+                    finish(fit(g, 3, h), g, 3, h)
+                    store(g, 3, h * HALF, (h + 1) * HALF)
+            if g + 2 < OBS_PASSES:
+                prescale(g + 2, 0)
+                prescale(g + 2, 1)

@@ -13,6 +13,7 @@ U8 = mybir.dt.uint8
 FP8X4 = mybir.dt.float8_e4m3fn_x4
 COPY = mybir.ActivationFunctionType.Copy
 MULT = mybir.AluOpType.mult
+ADD = mybir.AluOpType.add
 SUBTRACT = mybir.AluOpType.subtract
 
 P = 128
@@ -23,6 +24,7 @@ UNIT = 2048
 OBS_PASSES = N_OBS // K_PASS
 CTRL_PASSES = N_CTRL // K_PASS
 V_COLS = 384
+V_COLS_COEF = 320
 RUN = 4
 
 
@@ -37,7 +39,7 @@ def tile_shrunken_control_residuals_s7_kernel(tc, pinv, treat, controls, shrink,
         def bank(i):
             return psum.tile([P, HALF], F32, name="bank%d" % i)
 
-        pinv_raw = [keep.tile([P, UNIT], BF16, name="pinv_raw%d" % s) for s in range(2 * PACK)]
+        pinv_raw = [ring.tile([P, UNIT], BF16, name="unit_raw", bufs=2 * PACK) for s in range(2 * PACK)]
         treat_raw = [keep.tile([P, 2 * UNIT], BF16, name="treat_raw%d" % k) for k in range(OBS_PASSES)]
         ctrl_raw = [keep.tile([P, 2 * UNIT], BF16, name="ctrl_raw%d" % g) for g in range(OBS_PASSES)]
         shrink_bf = keep.tile([P, CTRL_PASSES, PACK], BF16, name="shrink_bf")
@@ -52,23 +54,32 @@ def tile_shrunken_control_residuals_s7_kernel(tc, pinv, treat, controls, shrink,
                 in_=treat[k * K_PASS:(k + 1) * K_PASS, h * HALF:(h + 1) * HALF].rearrange("(p t) j -> p t j", t=PACK),
             )
 
+        def load_pinv(s):
+            if s < PACK:
+                nc.sync.dma_start(
+                    out=pinv_raw[s][:].rearrange("p (t k) -> p t k", t=PACK),
+                    in_=pinv[0:K_PASS, s * K_PASS:(s + 1) * K_PASS].rearrange("(p t) k -> p t k", t=PACK),
+                )
+            else:
+                nc.sync.dma_start(
+                    out=pinv_raw[s][:],
+                    in_=pinv[K_PASS:2 * K_PASS, :].rearrange("(p t) k -> p t k", t=PACK)[:, s - PACK, :],
+                )
+
+        def load_controls(g, u):
+            rows = controls[g * K_PASS:(g + 1) * K_PASS, :].rearrange("(p t) c -> p (t c)", t=PACK)
+            nc.sync.dma_start(out=ctrl_raw[g][:, u * UNIT:(u + 1) * UNIT], in_=rows[:, u * UNIT:(u + 1) * UNIT])
+
         nc.scalar.dma_start(out=shrink_bf[:], in_=shrink.rearrange("(g p t) -> p g t", p=P, t=PACK))
         for k in range(OBS_PASSES):
-            nc.sync.dma_start(
-                out=pinv_raw[k][:].rearrange("p (t k) -> p t k", t=PACK),
-                in_=pinv[0:K_PASS, k * K_PASS:(k + 1) * K_PASS].rearrange("(p t) k -> p t k", t=PACK),
-            )
+            load_pinv(k)
             load_treat(k, 0)
         for t in range(PACK):
-            nc.sync.dma_start(
-                out=pinv_raw[PACK + t][:],
-                in_=pinv[K_PASS:2 * K_PASS, :].rearrange("(p t) k -> p t k", t=PACK)[:, t, :],
-            )
+            load_pinv(PACK + t)
             load_treat(t, 1)
         for g in range(OBS_PASSES):
-            rows = controls[g * K_PASS:(g + 1) * K_PASS, :].rearrange("(p t) c -> p (t c)", t=PACK)
             for u in range(2):
-                nc.sync.dma_start(out=ctrl_raw[g][:, u * UNIT:(u + 1) * UNIT], in_=rows[:, u * UNIT:(u + 1) * UNIT])
+                load_controls(g, u)
             if g == 0:
                 nc.sync.dma_start(out=sigma_bf[:], in_=sigma.rearrange("(g p t) -> p g t", p=P, t=PACK))
 
@@ -77,17 +88,25 @@ def tile_shrunken_control_residuals_s7_kernel(tc, pinv, treat, controls, shrink,
 
         mx = {}
 
-        def turn(raw, unit, banks):
-            words = raw[:, unit * UNIT:(unit + 1) * UNIT].bitcast(F32)
+        def sort_words(copy, raw):
+            tidy = ring.tile([P, UNIT], BF16, name="unit_raw", bufs=2 * PACK)
+            copy(
+                out=tidy[:].bitcast(F32).rearrange("p (q u m) -> p q u m", q=4, u=2),
+                in_=raw.bitcast(F32).rearrange("p (q m u) -> p q u m", q=4, u=2),
+            )
+            return tidy
+
+        def turn(raw, banks, is_sorted=False):
+            words = raw.bitcast(F32)
             held = [bank(i) for i in banks]
             for q in range(4):
                 for u in range(2):
                     slot = (q % 2) * 2 + u
-                    nc.tensor.transpose(
-                        held[q // 2][:, slot * P:(slot + 1) * P],
-                        words[:, 256 * q + u:256 * (q + 1):2],
-                        ident[:],
-                    )
+                    if is_sorted:
+                        source = words[:, 256 * q + P * u:256 * q + P * (u + 1)]
+                    else:
+                        source = words[:, 256 * q + u:256 * (q + 1):2]
+                    nc.tensor.transpose(held[q // 2][:, slot * P:(slot + 1) * P], source, ident[:])
             return held
 
         def unload(held):
@@ -136,7 +155,7 @@ def tile_shrunken_control_residuals_s7_kernel(tc, pinv, treat, controls, shrink,
 
         def shrink_out(acc, h, g, t, on_vector=False):
             if (h, g) not in coef_rows:
-                coef_rows[h, g] = ring.tile([P, UNIT], BF16, name="coef_rows", bufs=3)
+                coef_rows[h, g] = ring.tile([P, UNIT], BF16, name="coef_rows", bufs=2)
             dst = coef_rows[h, g][:, t * HALF:(t + 1) * HALF]
             factor = shrink_f[:, g * PACK + t:g * PACK + t + 1]
             if on_vector:
@@ -149,22 +168,33 @@ def tile_shrunken_control_residuals_s7_kernel(tc, pinv, treat, controls, shrink,
 
         result = {}
 
-        def prescale(g, t, on_vector=False):
-            res = ring.tile([P, N_TREAT], F32, name="result", bufs=9)
+        def negate_sigma(lo, hi):
+            nc.vector.tensor_scalar(
+                out=neg_sigma[:, lo:hi], in0=sigma_bf[:].rearrange("p g t -> p (g t)")[:, lo:hi],
+                scalar1=-1.0, scalar2=None, op0=MULT,
+            )
+
+        def prescale(g, t, engine):
+            res = ring.tile([P, N_TREAT], F32, name="result", bufs=10)
             result[g, t] = res
             src = treat_raw[g][:].rearrange("p (h t j) -> p h t j", h=2, t=PACK)[:, :, t, :]
             dst = res[:].rearrange("p (h j) -> p h j", h=2)
             factor = neg_sigma[:, g * PACK + t:g * PACK + t + 1]
-            if on_vector:
+            if engine == "vector":
                 nc.vector.tensor_scalar(out=dst, in0=src, scalar1=factor, scalar2=None, op0=MULT)
+            elif engine == "gpsimd":
+                nc.gpsimd.tensor_scalar(out=dst, in0=src, scalar1=factor, scalar2=0.0, op0=MULT, op1=ADD)
             else:
                 nc.scalar.activation(out=dst, in_=src, func=COPY, scale=factor)
 
         turns = [0]
 
-        def fit(g, t, h):
-            acc = bank(turns[0] % 4)
+        def next_bank():
             turns[0] = turns[0] + 1
+            return (turns[0] - 1) % 8
+
+        def fit(g, t, h):
+            acc = bank(next_bank())
             for c in range(CTRL_PASSES):
                 matmul(acc, ("ctrl", g, t // 2), (t % 2) * 2 + c, ("coef", h, c), c == 0, c == CTRL_PASSES - 1)
             return acc
@@ -190,97 +220,103 @@ def tile_shrunken_control_residuals_s7_kernel(tc, pinv, treat, controls, shrink,
             weave(nc.vector.tensor_copy, grouped, coef_rows[h, g][:], 0, HALF)
             return grouped
 
-        def coef_tile(h, g, t):
-            acc = bank(t)
+        def coef_tile(h, g, t, which):
+            acc = bank(which)
             for k in range(OBS_PASSES):
                 coef_pass(acc, h, g, t, k)
             return acc
 
-        def turn_controls(g):
-            return [turn(ctrl_raw[g], u, (4 + 2 * u, 5 + 2 * u)) for u in range(2)]
+        def ctrl_unit(g, u):
+            return ctrl_raw[g][:, u * UNIT:(u + 1) * UNIT]
+
+        def bank_pair(i):
+            return (4 + 2 * (i % 2), 5 + 2 * (i % 2))
 
         accs = [bank(t) for t in range(PACK)]
-        for s in range(2 * PACK):
-            held = turn(pinv_raw[s], 0, (4 + 2 * (s % 2), 5 + 2 * (s % 2)))
+        for s in range(2 * PACK + 2):
+            source = pinv_raw[s][:] if s < 2 * PACK else ctrl_unit(0, s - 2 * PACK)
+            held = turn(source, bank_pair(s))
             if 0 < s <= PACK:
                 for t in range(PACK):
                     coef_pass(accs[t], 0, 0, t, s - 1)
-            elif s > PACK:
-                acc = coef_tile(0, 1, s - PACK - 1)
+            elif PACK < s <= 2 * PACK:
+                acc = coef_tile(0, 1, s - PACK - 1, s - PACK - 1)
             turned = unload(held)
-            grouped = woven()
-            k, h = s % PACK, s // PACK
-            if h == 0:
-                weave(nc.vector.tensor_copy, grouped, treat_half(k, h), 0, V_COLS)
-                weave(nc.scalar.copy, grouped, treat_half(k, h), V_COLS, HALF)
+            if s < PACK:
+                grouped = woven()
+                weave(nc.vector.tensor_copy, grouped, treat_half(s, 0), 0, V_COLS)
+                weave(nc.scalar.copy, grouped, treat_half(s, 0), V_COLS, HALF)
+                quantise(("pinv", 0, s), turned)
+                quantise(("treat", 0, s), grouped)
+                continue
+            if s < 2 * PACK:
+                shrink_out(accs[s - PACK], 0, 0, s - PACK)
+            if PACK < s <= 2 * PACK:
+                shrink_out(acc, 0, 1, s - PACK - 1)
+            if s < 2 * PACK:
+                grouped = woven()
+                weave(nc.vector.tensor_copy, grouped, treat_half(s - PACK, 1), 0, HALF)
+                quantise(("pinv", 1, s - PACK), turned)
+                quantise(("treat", 1, s - PACK), grouped)
             else:
-                weave(nc.vector.tensor_copy, grouped, treat_half(k, h), 0, HALF)
-                shrink_out(accs[k], 0, 0, k)
-                if s > PACK:
-                    shrink_out(acc, 0, 1, k - 1)
-            quantise(("pinv", h, k), turned)
-            quantise(("treat", h, k), grouped)
-        held = turn_controls(0)
-        acc = coef_tile(0, 1, PACK - 1)
-        turned = [unload(held[u]) for u in range(2)]
-        shrink_out(acc, 0, 1, PACK - 1)
-        nc.scalar.activation(out=neg_sigma[:], in_=sigma_bf[:].rearrange("p g t -> p (g t)"), func=COPY, scale=-1.0)
+                if s == 2 * PACK:
+                    negate_sigma(0, 5)
+                grouped = weave_coef(0, s - 2 * PACK)
+                quantise(("ctrl", 0, s - 2 * PACK), turned, "ctrl", 4)
+                quantise(("coef", 0, s - 2 * PACK), grouped)
 
-        first = weave_coef(0, 0)
-        quantise(("ctrl", 0, 0), turned[0], "ctrl", 4)
-        quantise(("coef", 0, 0), first)
-        second = weave_coef(0, 1)
-        quantise(("ctrl", 0, 1), turned[1], "ctrl", 4)
-        quantise(("coef", 0, 1), second)
+        tidy = {}
         for t in range(PACK):
-            shrink_out(coef_tile(1, 0, t), 1, 0, t)
-        prescale(0, 0, on_vector=True)
+            shrink_out(coef_tile(1, 0, t, next_bank()), 1, 0, t)
+            if t % 3 == 0:
+                prescale(0, t // 3, "scalar")
+        for u in range(2):
+            tidy[1, u] = sort_words(nc.vector.tensor_copy, ctrl_unit(1, u))
+            prescale(0, 2 + u, "vector")
         first = weave_coef(1, 0)
-        prescale(0, 1, on_vector=True)
+        tidy[2, 0] = sort_words(nc.vector.tensor_copy, ctrl_unit(2, 0))
         quantise(("coef", 1, 0), first)
-        prescale(0, 2, on_vector=True)
-        prescale(0, 3, on_vector=True)
+        tidy[2, 1] = sort_words(nc.vector.tensor_copy, ctrl_unit(2, 1))
         for t in range(PACK):
-            shrink_out(coef_tile(1, 1, t), 1, 1, t)
-            if t == 0:
-                prescale(1, 0)
+            shrink_out(coef_tile(1, 1, t, next_bank()), 1, 1, t)
+            if t == 1:
+                prescale(1, 0, "scalar")
 
         accs = [fit(0, t, 0) for t in range(PACK)]
-        second = weave_coef(1, 1)
-        prescale(1, 1)
+        second = woven()
+        weave(nc.vector.tensor_copy, second, coef_rows[1, 1][:], 0, V_COLS_COEF)
+        weave(nc.scalar.copy, second, coef_rows[1, 1][:], V_COLS_COEF, HALF)
         for t in range(PACK):
             finish(accs[t], 0, t, 0)
             store(0, t, 0, HALF)
             if t == 0:
                 quantise(("coef", 1, 1), second)
+                negate_sigma(5, 6)
+                prescale(1, 1, "gpsimd")
         for g in range(OBS_PASSES):
             more = g + 1 < OBS_PASSES
             if g > 0:
                 tile_out(g, 0)
                 tile_out(g, 1)
             if more:
-                turned = [unload(pair) for pair in turn_controls(g + 1)]
+                held = [turn(tidy[g + 1, u][:], (next_bank(), next_bank()), is_sorted=True) for u in range(2)]
+                turned = [unload(pair) for pair in held]
                 quantise(("ctrl", g + 1, 0), turned[0], "ctrl", 4)
-                prescale(g + 1, 2)
-                prescale(g + 1, 3)
-            if g > 0:
-                tile_out(g, 2)
-            else:
-                for t in range(2):
-                    finish(fit(g, t, 1), g, t, 1)
-                    store(g, t, HALF, N_TREAT)
-            if more:
-                quantise(("ctrl", g + 1, 1), turned[1], "ctrl", 4)
             if g == 0:
-                for t in range(2, 4):
-                    finish(fit(g, t, 1), g, t, 1)
-                    store(g, t, HALF, N_TREAT)
-            elif more:
-                tile_out(g, 3)
-            else:
+                for u in range(2):
+                    tidy[3, u] = sort_words(nc.scalar.copy, ctrl_unit(3, u))
+            for t in range(2, 4):
                 for h in range(2):
-                    finish(fit(g, 3, h), g, 3, h)
-                    store(g, 3, h * HALF, (h + 1) * HALF)
-            if g + 2 < OBS_PASSES:
-                prescale(g + 2, 0)
-                prescale(g + 2, 1)
+                    tt, hh = (t, h) if g > 0 else (2 * (t - 2) + h, 1)
+                    finish(fit(g, tt, hh), g, tt, hh)
+                    if g == 0 or (not more and t == 3):
+                        store(g, tt, hh * HALF, (hh + 1) * HALF)
+                    elif h == 1:
+                        store(g, tt, 0, N_TREAT)
+                    if more and t == 2 and h == 0:
+                        quantise(("ctrl", g + 1, 1), turned[1], "ctrl", 4)
+                        lo = PACK * (g + 1) + 2
+                        hi = min(lo + PACK, OBS_PASSES * PACK)
+                        negate_sigma(lo, hi)
+                        for i in range(lo, hi):
+                            prescale(i // PACK, i % PACK, "gpsimd" if i < lo + 3 else "scalar")

@@ -20,12 +20,16 @@ P = 128
 PACK = 4
 K_PASS = P * PACK
 HALF = 512
-UNIT = 2048
-OBS_PASSES = N_OBS // K_PASS
-CTRL_PASSES = N_CTRL // K_PASS
-V_COLS = 384
-V_COLS_COEF = 320
+UNIT = PACK * HALF
+PASS_WORDS = K_PASS // 2
+OBS_GROUPS = N_OBS // K_PASS
+CTRL_GROUPS = N_CTRL // K_PASS
+BANKS = 8
 RUN = 4
+VECTOR_COLS_TREAT = 384
+VECTOR_COLS_COEF = 320
+GPSIMD_PRESCALES = 3
+RESULT_TILES = 2 * PACK + 2
 
 
 def tile_shrunken_control_residuals_s7_kernel(tc, pinv, treat, controls, shrink, sigma, out):
@@ -36,107 +40,114 @@ def tile_shrunken_control_residuals_s7_kernel(tc, pinv, treat, controls, shrink,
         psum = ctx.enter_context(tc.psum_pool(name="psum", bufs=1))
         ctx.enter_context(tc.manual_schedule())
 
-        def bank(i):
-            return psum.tile([P, HALF], F32, name="bank%d" % i)
+        def raw_unit():
+            return ring.tile([P, UNIT], BF16, name="raw_unit", bufs=2 * PACK)
 
-        pinv_raw = [ring.tile([P, UNIT], BF16, name="unit_raw", bufs=2 * PACK) for s in range(2 * PACK)]
-        treat_raw = [keep.tile([P, 2 * UNIT], BF16, name="treat_raw%d" % k) for k in range(OBS_PASSES)]
-        ctrl_raw = [keep.tile([P, 2 * UNIT], BF16, name="ctrl_raw%d" % g) for g in range(OBS_PASSES)]
-        shrink_bf = keep.tile([P, CTRL_PASSES, PACK], BF16, name="shrink_bf")
-        shrink_f = keep.tile([P, CTRL_PASSES * PACK], F32, name="shrink_f")
-        sigma_bf = keep.tile([P, OBS_PASSES, PACK], BF16, name="sigma_bf")
-        neg_sigma = keep.tile([P, OBS_PASSES * PACK], F32, name="neg_sigma")
+        pinv_raw = [raw_unit() for s in range(2 * PACK)]
+        treat_raw = [keep.tile([P, 2 * UNIT], BF16, name="treat_raw%d" % g) for g in range(OBS_GROUPS)]
+        ctrl_raw = [keep.tile([P, 2 * UNIT], BF16, name="ctrl_raw%d" % g) for g in range(OBS_GROUPS)]
+        shrink_bf = keep.tile([P, CTRL_GROUPS, PACK], BF16, name="shrink_bf")
+        shrink_f32 = keep.tile([P, CTRL_GROUPS * PACK], F32, name="shrink_f32")
+        sigma_bf = keep.tile([P, OBS_GROUPS, PACK], BF16, name="sigma_bf")
+        neg_sigma = keep.tile([P, OBS_GROUPS * PACK], F32, name="neg_sigma")
         ident = keep.tile([P, P], F32, name="ident")
 
-        def load_treat(k, h):
-            nc.sync.dma_start(
-                out=treat_raw[k][:, h * UNIT:(h + 1) * UNIT].rearrange("p (t j) -> p t j", t=PACK),
-                in_=treat[k * K_PASS:(k + 1) * K_PASS, h * HALF:(h + 1) * HALF].rearrange("(p t) j -> p t j", t=PACK),
-            )
+        def treat_unit(g, h):
+            return treat_raw[g][:, h * UNIT:(h + 1) * UNIT]
 
-        def load_pinv(s):
-            if s < PACK:
+        def ctrl_unit(g, pair):
+            return ctrl_raw[g][:, pair * UNIT:(pair + 1) * UNIT]
+
+        nc.scalar.dma_start(out=shrink_bf[:], in_=shrink.rearrange("(g p t) -> p g t", p=P, t=PACK))
+        for s in range(2 * PACK):
+            h, i = divmod(s, PACK)
+            if h == 0:
                 nc.sync.dma_start(
                     out=pinv_raw[s][:].rearrange("p (t k) -> p t k", t=PACK),
-                    in_=pinv[0:K_PASS, s * K_PASS:(s + 1) * K_PASS].rearrange("(p t) k -> p t k", t=PACK),
+                    in_=pinv[0:K_PASS, i * K_PASS:(i + 1) * K_PASS].rearrange("(p t) k -> p t k", t=PACK),
                 )
             else:
                 nc.sync.dma_start(
                     out=pinv_raw[s][:],
-                    in_=pinv[K_PASS:2 * K_PASS, :].rearrange("(p t) k -> p t k", t=PACK)[:, s - PACK, :],
+                    in_=pinv[K_PASS:2 * K_PASS, :].rearrange("(p t) k -> p t k", t=PACK)[:, i, :],
                 )
-
-        def load_controls(g, u):
+            nc.sync.dma_start(
+                out=treat_unit(i, h).rearrange("p (t j) -> p t j", t=PACK),
+                in_=treat[i * K_PASS:(i + 1) * K_PASS, h * HALF:(h + 1) * HALF].rearrange("(p t) j -> p t j", t=PACK),
+            )
+        for g in range(OBS_GROUPS):
             rows = controls[g * K_PASS:(g + 1) * K_PASS, :].rearrange("(p t) c -> p (t c)", t=PACK)
-            nc.sync.dma_start(out=ctrl_raw[g][:, u * UNIT:(u + 1) * UNIT], in_=rows[:, u * UNIT:(u + 1) * UNIT])
-
-        nc.scalar.dma_start(out=shrink_bf[:], in_=shrink.rearrange("(g p t) -> p g t", p=P, t=PACK))
-        for k in range(OBS_PASSES):
-            load_pinv(k)
-            load_treat(k, 0)
-        for t in range(PACK):
-            load_pinv(PACK + t)
-            load_treat(t, 1)
-        for g in range(OBS_PASSES):
-            for u in range(2):
-                load_controls(g, u)
+            for pair in range(2):
+                nc.sync.dma_start(out=ctrl_unit(g, pair), in_=rows[:, pair * UNIT:(pair + 1) * UNIT])
             if g == 0:
                 nc.sync.dma_start(out=sigma_bf[:], in_=sigma.rearrange("(g p t) -> p g t", p=P, t=PACK))
 
         make_identity(nc, ident[:])
-        nc.scalar.activation(out=shrink_f[:], in_=shrink_bf[:].rearrange("p g t -> p (g t)"), func=COPY)
+        nc.scalar.activation(out=shrink_f32[:], in_=shrink_bf[:].rearrange("p g t -> p (g t)"), func=COPY)
 
         mx = {}
+        coef_rows = {}
+        result = {}
+        banks_taken = [0]
+
+        def bank(i):
+            return psum.tile([P, HALF], F32, name="bank%d" % i)
+
+        def next_bank():
+            banks_taken[0] = banks_taken[0] + 1
+            return bank((banks_taken[0] - 1) % BANKS)
 
         def sort_words(copy, raw):
-            tidy = ring.tile([P, UNIT], BF16, name="unit_raw", bufs=2 * PACK)
+            tidy = raw_unit()
             copy(
-                out=tidy[:].bitcast(F32).rearrange("p (q u m) -> p q u m", q=4, u=2),
-                in_=raw.bitcast(F32).rearrange("p (q m u) -> p q u m", q=4, u=2),
+                out=tidy[:].bitcast(F32).rearrange("p (q u m) -> p q u m", q=PACK, u=2),
+                in_=raw.bitcast(F32).rearrange("p (q m u) -> p q u m", q=PACK, u=2),
             )
             return tidy
 
-        def turn(raw, banks, is_sorted=False):
-            words = raw.bitcast(F32)
-            held = [bank(i) for i in banks]
-            for q in range(4):
+        def turn(raw, held, is_sorted):
+            words = raw[:].bitcast(F32)
+            for q in range(PACK):
                 for u in range(2):
-                    slot = (q % 2) * 2 + u
+                    base = PASS_WORDS * q
                     if is_sorted:
-                        source = words[:, 256 * q + P * u:256 * q + P * (u + 1)]
+                        source = words[:, base + P * u:base + P * (u + 1)]
                     else:
-                        source = words[:, 256 * q + u:256 * (q + 1):2]
-                    nc.tensor.transpose(held[q // 2][:, slot * P:(slot + 1) * P], source, ident[:])
+                        source = words[:, base + u:base + PASS_WORDS:2]
+                    place = (q % 2) * 2 + u
+                    nc.tensor.transpose(held[q // 2][:, place * P:(place + 1) * P], source, ident[:])
             return held
 
         def unload(held):
-            grouped = ring.tile([P, UNIT], BF16, name="turned", bufs=3, align_bytes=64)
-            words = grouped[:].bitcast(F32)
+            turned = ring.tile([P, UNIT], BF16, name="turned", bufs=3, align_bytes=64)
+            words = turned[:].bitcast(F32)
             for b in range(2):
                 nc.scalar.copy(
                     out=words[:, b * HALF:(b + 1) * HALF].rearrange("p (q m u) -> p q m u", q=2, u=2),
                     in_=held[b][:].rearrange("p (q u m) -> p q m u", q=2, u=2),
                 )
-            return grouped
+            return turned
 
-        def quantise(key, grouped, tag=None, bufs=1):
-            name = tag or "%s_%d_%d" % key
-            codes = keep.tile([P, HALF], U32, name="c_" + name, bufs=bufs, align_bytes=64)
-            scales = keep.tile([P, HALF], U8, name="s_" + name, bufs=bufs, align_bytes=64)
-            nc.vector.quantize_mx(out=codes[:].bitcast(FP8X4), scales=scales[:], in_=grouped[:])
+        def weave(rows, vector_cols=HALF):
+            woven = ring.tile([P, UNIT], BF16, name="woven", bufs=3, align_bytes=64)
+            for copy, lo, hi in ((nc.vector.tensor_copy, 0, vector_cols), (nc.scalar.copy, vector_cols, HALF)):
+                if lo < hi:
+                    copy(
+                        out=woven[:, PACK * lo:PACK * hi].rearrange("p (c i t) -> p c t i", i=RUN, t=PACK),
+                        in_=rows.rearrange("p (t j) -> p t j", t=PACK)[:, :, lo:hi].rearrange(
+                            "p t (c i) -> p c t i", i=RUN),
+                    )
+            return woven
+
+        def quantise(key, unit):
+            name, bufs = ("ctrl", 4) if key[0] == "ctrl" else ("%s_%d_%d" % key, 1)
+            codes = keep.tile([P, HALF], U32, name="codes_" + name, bufs=bufs, align_bytes=64)
+            scales = keep.tile([P, HALF], U8, name="scales_" + name, bufs=bufs, align_bytes=64)
+            nc.vector.quantize_mx(out=codes[:].bitcast(FP8X4), scales=scales[:], in_=unit[:])
             mx[key] = (codes, scales)
 
-        def weave(copy, grouped, rows, lo, hi):
-            copy(
-                out=grouped[:, PACK * lo:PACK * hi].rearrange("p (c i t) -> p c t i", i=RUN, t=PACK),
-                in_=rows.rearrange("p (t j) -> p t j", t=PACK)[:, :, lo:hi].rearrange("p t (c i) -> p c t i", i=RUN),
-            )
-
-        def woven():
-            return ring.tile([P, UNIT], BF16, name="woven", bufs=3, align_bytes=64)
-
-        def matmul(acc, left, block, right, start, stop):
-            cols = slice(block * P, (block + 1) * P)
+        def matmul(acc, left, quarter, right, start, stop):
+            cols = slice(quarter * P, (quarter + 1) * P)
             nc.tensor.matmul_mx(
                 out=acc[:],
                 lhsT=mx[left][0][:, cols].bitcast(FP8X4),
@@ -148,25 +159,21 @@ def tile_shrunken_control_residuals_s7_kernel(tc, pinv, treat, controls, shrink,
             )
 
         def coef_pass(acc, h, g, t, k):
-            left, block = (("pinv", 0, k), t) if g == 0 else (("pinv", 1, t), k)
-            matmul(acc, left, block, ("treat", h, k), k == 0, k == OBS_PASSES - 1)
+            left, quarter = (("pinv", 0, k), t) if g == 0 else (("pinv", 1, t), k)
+            matmul(acc, left, quarter, ("treat", h, k), k == 0, k == OBS_GROUPS - 1)
 
-        coef_rows = {}
+        def coef_tile(acc, h, g, t):
+            for k in range(OBS_GROUPS):
+                coef_pass(acc, h, g, t, k)
+            return acc
 
-        def shrink_out(acc, h, g, t, on_vector=False):
-            if (h, g) not in coef_rows:
-                coef_rows[h, g] = ring.tile([P, UNIT], BF16, name="coef_rows", bufs=2)
-            dst = coef_rows[h, g][:, t * HALF:(t + 1) * HALF]
-            factor = shrink_f[:, g * PACK + t:g * PACK + t + 1]
-            if on_vector:
-                nc.vector.tensor_scalar(out=dst, in0=acc[:], scalar1=factor, scalar2=None, op0=MULT)
-            else:
-                nc.scalar.activation(out=dst, in_=acc[:], func=COPY, scale=factor)
-
-        def treat_half(k, h):
-            return treat_raw[k][:, h * UNIT:(h + 1) * UNIT]
-
-        result = {}
+        def shrink_out(acc, h, g, t):
+            if t == 0:
+                coef_rows[h, g] = ring.tile([P, UNIT], BF16, name="coef_rows")
+            nc.scalar.activation(
+                out=coef_rows[h, g][:, t * HALF:(t + 1) * HALF], in_=acc[:], func=COPY,
+                scale=shrink_f32[:, g * PACK + t:g * PACK + t + 1],
+            )
 
         def negate_sigma(lo, hi):
             nc.vector.tensor_scalar(
@@ -175,10 +182,9 @@ def tile_shrunken_control_residuals_s7_kernel(tc, pinv, treat, controls, shrink,
             )
 
         def prescale(g, t, engine):
-            res = ring.tile([P, N_TREAT], F32, name="result", bufs=10)
-            result[g, t] = res
+            result[g, t] = ring.tile([P, N_TREAT], F32, name="result", bufs=RESULT_TILES)
             src = treat_raw[g][:].rearrange("p (h t j) -> p h t j", h=2, t=PACK)[:, :, t, :]
-            dst = res[:].rearrange("p (h j) -> p h j", h=2)
+            dst = result[g, t][:].rearrange("p (h j) -> p h j", h=2)
             factor = neg_sigma[:, g * PACK + t:g * PACK + t + 1]
             if engine == "vector":
                 nc.vector.tensor_scalar(out=dst, in0=src, scalar1=factor, scalar2=None, op0=MULT)
@@ -187,16 +193,10 @@ def tile_shrunken_control_residuals_s7_kernel(tc, pinv, treat, controls, shrink,
             else:
                 nc.scalar.activation(out=dst, in_=src, func=COPY, scale=factor)
 
-        turns = [0]
-
-        def next_bank():
-            turns[0] = turns[0] + 1
-            return (turns[0] - 1) % 8
-
         def fit(g, t, h):
-            acc = bank(next_bank())
-            for c in range(CTRL_PASSES):
-                matmul(acc, ("ctrl", g, t // 2), (t % 2) * 2 + c, ("coef", h, c), c == 0, c == CTRL_PASSES - 1)
+            acc = next_bank()
+            for c in range(CTRL_GROUPS):
+                matmul(acc, ("ctrl", g, t // 2), (t % 2) * 2 + c, ("coef", h, c), c == 0, c == CTRL_GROUPS - 1)
             return acc
 
         def finish(acc, g, t, h):
@@ -210,113 +210,93 @@ def tile_shrunken_control_residuals_s7_kernel(tc, pinv, treat, controls, shrink,
             rows = out[g * K_PASS:(g + 1) * K_PASS, :].rearrange("(p t) j -> p t j", t=PACK)
             nc.sync.dma_start(out=rows[:, t, lo:hi], in_=result[g, t][:, lo:hi])
 
-        def tile_out(g, t):
-            for h in range(2):
-                finish(fit(g, t, h), g, t, h)
-            store(g, t, 0, N_TREAT)
+        def turn_controls(g):
+            held = [turn(tidy[g, pair], (next_bank(), next_bank()), True) for pair in range(2)]
+            return [unload(two) for two in held]
 
-        def weave_coef(h, g):
-            grouped = woven()
-            weave(nc.vector.tensor_copy, grouped, coef_rows[h, g][:], 0, HALF)
-            return grouped
-
-        def coef_tile(h, g, t, which):
-            acc = bank(which)
-            for k in range(OBS_PASSES):
-                coef_pass(acc, h, g, t, k)
-            return acc
-
-        def ctrl_unit(g, u):
-            return ctrl_raw[g][:, u * UNIT:(u + 1) * UNIT]
-
-        def bank_pair(i):
-            return (4 + 2 * (i % 2), 5 + 2 * (i % 2))
-
-        accs = [bank(t) for t in range(PACK)]
-        for s in range(2 * PACK + 2):
-            source = pinv_raw[s][:] if s < 2 * PACK else ctrl_unit(0, s - 2 * PACK)
-            held = turn(source, bank_pair(s))
+        sums = [bank(2 + t) for t in range(PACK)]
+        for s in range(2 * PACK):
+            h, i = divmod(s, PACK)
+            held = turn(pinv_raw[s], [bank(b) for b in ((0, 1), (6, 7))[s % 2]], False)
             if 0 < s <= PACK:
                 for t in range(PACK):
-                    coef_pass(accs[t], 0, 0, t, s - 1)
-            elif PACK < s <= 2 * PACK:
-                acc = coef_tile(0, 1, s - PACK - 1, s - PACK - 1)
+                    coef_pass(sums[t], 0, 0, t, s - 1)
+            elif s > PACK:
+                acc = coef_tile(bank(2 + i - 1), 0, 1, i - 1)
             turned = unload(held)
-            if s < PACK:
-                grouped = woven()
-                weave(nc.vector.tensor_copy, grouped, treat_half(s, 0), 0, V_COLS)
-                weave(nc.scalar.copy, grouped, treat_half(s, 0), V_COLS, HALF)
-                quantise(("pinv", 0, s), turned)
-                quantise(("treat", 0, s), grouped)
-                continue
-            if s < 2 * PACK:
-                shrink_out(accs[s - PACK], 0, 0, s - PACK)
-            if PACK < s <= 2 * PACK:
-                shrink_out(acc, 0, 1, s - PACK - 1)
-            if s < 2 * PACK:
-                grouped = woven()
-                weave(nc.vector.tensor_copy, grouped, treat_half(s - PACK, 1), 0, HALF)
-                quantise(("pinv", 1, s - PACK), turned)
-                quantise(("treat", 1, s - PACK), grouped)
+            if h == 0:
+                woven = weave(treat_unit(i, h), VECTOR_COLS_TREAT)
             else:
-                if s == 2 * PACK:
-                    negate_sigma(0, 5)
-                grouped = weave_coef(0, s - 2 * PACK)
-                quantise(("ctrl", 0, s - 2 * PACK), turned, "ctrl", 4)
-                quantise(("coef", 0, s - 2 * PACK), grouped)
+                shrink_out(sums[i], 0, 0, i)
+                if i > 0:
+                    shrink_out(acc, 0, 1, i - 1)
+                woven = weave(treat_unit(i, h))
+            quantise(("pinv", h, i), turned)
+            quantise(("treat", h, i), woven)
 
         tidy = {}
+        for pair in range(2):
+            tidy[0, pair] = sort_words(nc.scalar.copy, ctrl_unit(0, pair))
+        early = [next_bank() for t in range(2)]
+        for k in range(OBS_GROUPS - 1):
+            for t in range(2):
+                coef_pass(early[t], 1, 0, t, k)
+        shrink_out(coef_tile(bank(2 + PACK - 1), 0, 1, PACK - 1), 0, 1, PACK - 1)
+        for t in range(2):
+            coef_pass(early[t], 1, 0, t, OBS_GROUPS - 1)
+            shrink_out(early[t], 1, 0, t)
+        negate_sigma(0, PACK + 2)
+        for g in range(CTRL_GROUPS):
+            woven = weave(coef_rows[0, g][:])
+            prescale(0, 2 * g, "vector")
+            quantise(("coef", 0, g), woven)
+            prescale(0, 2 * g + 1, "vector")
+        for t in range(2, PACK):
+            shrink_out(coef_tile(next_bank(), 1, 0, t), 1, 0, t)
+        turned = turn_controls(0)
+        woven = weave(coef_rows[1, 0][:])
+        tidy[1, 0] = sort_words(nc.vector.tensor_copy, ctrl_unit(1, 0))
+        quantise(("coef", 1, 0), woven)
+        for pair in range(2):
+            quantise(("ctrl", 0, pair), turned[pair])
+        tidy[1, 1] = sort_words(nc.vector.tensor_copy, ctrl_unit(1, 1))
+        prescale(1, 1, "vector")
         for t in range(PACK):
-            shrink_out(coef_tile(1, 0, t, next_bank()), 1, 0, t)
-            if t % 3 == 0:
-                prescale(0, t // 3, "scalar")
-        for u in range(2):
-            tidy[1, u] = sort_words(nc.vector.tensor_copy, ctrl_unit(1, u))
-            prescale(0, 2 + u, "vector")
-        first = weave_coef(1, 0)
-        tidy[2, 0] = sort_words(nc.vector.tensor_copy, ctrl_unit(2, 0))
-        quantise(("coef", 1, 0), first)
-        tidy[2, 1] = sort_words(nc.vector.tensor_copy, ctrl_unit(2, 1))
-        for t in range(PACK):
-            shrink_out(coef_tile(1, 1, t, next_bank()), 1, 1, t)
-            if t == 1:
+            shrink_out(coef_tile(next_bank(), 1, 1, t), 1, 1, t)
+            if t == 0:
                 prescale(1, 0, "scalar")
 
-        accs = [fit(0, t, 0) for t in range(PACK)]
-        second = woven()
-        weave(nc.vector.tensor_copy, second, coef_rows[1, 1][:], 0, V_COLS_COEF)
-        weave(nc.scalar.copy, second, coef_rows[1, 1][:], V_COLS_COEF, HALF)
+        sums = [fit(0, t, 0) for t in range(PACK)]
+        woven = weave(coef_rows[1, 1][:], VECTOR_COLS_COEF)
         for t in range(PACK):
-            finish(accs[t], 0, t, 0)
+            finish(sums[t], 0, t, 0)
             store(0, t, 0, HALF)
             if t == 0:
-                quantise(("coef", 1, 1), second)
-                negate_sigma(5, 6)
-                prescale(1, 1, "gpsimd")
-        for g in range(OBS_PASSES):
-            more = g + 1 < OBS_PASSES
+                quantise(("coef", 1, 1), woven)
+        for g in range(OBS_GROUPS):
+            more = g + 1 < OBS_GROUPS
             if g > 0:
-                tile_out(g, 0)
-                tile_out(g, 1)
+                for t in range(2):
+                    for h in range(2):
+                        finish(fit(g, t, h), g, t, h)
+                    store(g, t, 0, N_TREAT)
             if more:
-                held = [turn(tidy[g + 1, u][:], (next_bank(), next_bank()), is_sorted=True) for u in range(2)]
-                turned = [unload(pair) for pair in held]
-                quantise(("ctrl", g + 1, 0), turned[0], "ctrl", 4)
-            if g == 0:
-                for u in range(2):
-                    tidy[3, u] = sort_words(nc.scalar.copy, ctrl_unit(3, u))
-            for t in range(2, 4):
-                for h in range(2):
-                    tt, hh = (t, h) if g > 0 else (2 * (t - 2) + h, 1)
-                    finish(fit(g, tt, hh), g, tt, hh)
-                    if g == 0 or (not more and t == 3):
-                        store(g, tt, hh * HALF, (hh + 1) * HALF)
-                    elif h == 1:
-                        store(g, tt, 0, N_TREAT)
-                    if more and t == 2 and h == 0:
-                        quantise(("ctrl", g + 1, 1), turned[1], "ctrl", 4)
-                        lo = PACK * (g + 1) + 2
-                        hi = min(lo + PACK, OBS_PASSES * PACK)
-                        negate_sigma(lo, hi)
-                        for i in range(lo, hi):
-                            prescale(i // PACK, i % PACK, "gpsimd" if i < lo + 3 else "scalar")
+                turned = turn_controls(g + 1)
+                quantise(("ctrl", g + 1, 0), turned[0])
+            if g + 2 < OBS_GROUPS:
+                for pair in range(2):
+                    tidy[g + 2, pair] = sort_words(nc.scalar.copy, ctrl_unit(g + 2, pair))
+            rest = [(t, 1) for t in range(PACK)] if g == 0 else [(t, h) for t in range(2, PACK) for h in range(2)]
+            for i, (t, h) in enumerate(rest):
+                finish(fit(g, t, h), g, t, h)
+                if g == 0 or (not more and t == PACK - 1):
+                    store(g, t, h * HALF, (h + 1) * HALF)
+                elif h == 1:
+                    store(g, t, 0, N_TREAT)
+                if more and i == 0:
+                    quantise(("ctrl", g + 1, 1), turned[1])
+                    lo = PACK * (g + 1) + 2
+                    hi = min(lo + PACK, OBS_GROUPS * PACK)
+                    negate_sigma(lo, hi)
+                    for r in range(lo, hi):
+                        prescale(r // PACK, r % PACK, "gpsimd" if r < lo + GPSIMD_PRESCALES else "scalar")

from contextlib import ExitStack

import concourse.mybir as mybir
from concourse.masks import make_identity

N_OBS, N_CTRL, N_TREAT = 2048, 1024, 1024
FLOPS = 2 * N_CTRL * N_OBS * N_TREAT + 2 * N_OBS * N_CTRL * N_TREAT

F32 = mybir.dt.float32
BF16 = mybir.dt.bfloat16
U32 = mybir.dt.uint32
U8 = mybir.dt.uint8
FP8X4 = mybir.dt.float8_e4m3fn_x4
COPY = mybir.ActivationFunctionType.Copy
MULT = mybir.AluOpType.mult
ADD = mybir.AluOpType.add
SUBTRACT = mybir.AluOpType.subtract

P = 128
PACK = 4
K_PASS = P * PACK
HALF = 512
UNIT = PACK * HALF
PASS_WORDS = K_PASS // 2
OBS_GROUPS = N_OBS // K_PASS
CTRL_GROUPS = N_CTRL // K_PASS
BANKS = 8
RUN = 4
VECTOR_COLS_TREAT = 384
VECTOR_COLS_COEF = 320
GPSIMD_PRESCALES = 3
RESULT_TILES = 2 * PACK + 2


def tile_shrunken_control_residuals_s7_kernel(tc, pinv, treat, controls, shrink, sigma, out):
    nc = tc.nc
    with ExitStack() as ctx:
        keep = ctx.enter_context(tc.tile_pool(name="keep", bufs=1))
        ring = ctx.enter_context(tc.tile_pool(name="ring", bufs=2))
        psum = ctx.enter_context(tc.psum_pool(name="psum", bufs=1))
        ctx.enter_context(tc.manual_schedule())

        def raw_unit():
            return ring.tile([P, UNIT], BF16, name="raw_unit", bufs=2 * PACK)

        pinv_raw = [raw_unit() for s in range(2 * PACK)]
        treat_raw = [keep.tile([P, 2 * UNIT], BF16, name="treat_raw%d" % g) for g in range(OBS_GROUPS)]
        ctrl_raw = [keep.tile([P, 2 * UNIT], BF16, name="ctrl_raw%d" % g) for g in range(OBS_GROUPS)]
        shrink_bf = keep.tile([P, CTRL_GROUPS, PACK], BF16, name="shrink_bf")
        shrink_f32 = keep.tile([P, CTRL_GROUPS * PACK], F32, name="shrink_f32")
        sigma_bf = keep.tile([P, OBS_GROUPS, PACK], BF16, name="sigma_bf")
        neg_sigma = keep.tile([P, OBS_GROUPS * PACK], F32, name="neg_sigma")
        ident = keep.tile([P, P], F32, name="ident")

        def treat_unit(g, h):
            return treat_raw[g][:, h * UNIT:(h + 1) * UNIT]

        def ctrl_unit(g, pair):
            return ctrl_raw[g][:, pair * UNIT:(pair + 1) * UNIT]

        nc.scalar.dma_start(out=shrink_bf[:], in_=shrink.rearrange("(g p t) -> p g t", p=P, t=PACK))
        for s in range(2 * PACK):
            h, i = divmod(s, PACK)
            if h == 0:
                nc.sync.dma_start(
                    out=pinv_raw[s][:].rearrange("p (t k) -> p t k", t=PACK),
                    in_=pinv[0:K_PASS, i * K_PASS:(i + 1) * K_PASS].rearrange("(p t) k -> p t k", t=PACK),
                )
            else:
                nc.sync.dma_start(
                    out=pinv_raw[s][:],
                    in_=pinv[K_PASS:2 * K_PASS, :].rearrange("(p t) k -> p t k", t=PACK)[:, i, :],
                )
            nc.sync.dma_start(
                out=treat_unit(i, h).rearrange("p (t j) -> p t j", t=PACK),
                in_=treat[i * K_PASS:(i + 1) * K_PASS, h * HALF:(h + 1) * HALF].rearrange("(p t) j -> p t j", t=PACK),
            )
        for g in range(OBS_GROUPS):
            rows = controls[g * K_PASS:(g + 1) * K_PASS, :].rearrange("(p t) c -> p (t c)", t=PACK)
            for pair in range(2):
                nc.sync.dma_start(out=ctrl_unit(g, pair), in_=rows[:, pair * UNIT:(pair + 1) * UNIT])
            if g == 0:
                nc.sync.dma_start(out=sigma_bf[:], in_=sigma.rearrange("(g p t) -> p g t", p=P, t=PACK))

        make_identity(nc, ident[:])
        nc.scalar.activation(out=shrink_f32[:], in_=shrink_bf[:].rearrange("p g t -> p (g t)"), func=COPY)

        mx = {}
        coef_rows = {}
        result = {}
        banks_taken = [0]

        def bank(i):
            return psum.tile([P, HALF], F32, name="bank%d" % i)

        def next_bank():
            banks_taken[0] = banks_taken[0] + 1
            return bank((banks_taken[0] - 1) % BANKS)

        def sort_words(copy, raw):
            tidy = raw_unit()
            copy(
                out=tidy[:].bitcast(F32).rearrange("p (q u m) -> p q u m", q=PACK, u=2),
                in_=raw.bitcast(F32).rearrange("p (q m u) -> p q u m", q=PACK, u=2),
            )
            return tidy

        def turn(raw, held, is_sorted):
            words = raw[:].bitcast(F32)
            for q in range(PACK):
                for u in range(2):
                    base = PASS_WORDS * q
                    if is_sorted:
                        source = words[:, base + P * u:base + P * (u + 1)]
                    else:
                        source = words[:, base + u:base + PASS_WORDS:2]
                    place = (q % 2) * 2 + u
                    nc.tensor.transpose(held[q // 2][:, place * P:(place + 1) * P], source, ident[:])
            return held

        def unload(held):
            turned = ring.tile([P, UNIT], BF16, name="turned", bufs=3, align_bytes=64)
            words = turned[:].bitcast(F32)
            for b in range(2):
                nc.scalar.copy(
                    out=words[:, b * HALF:(b + 1) * HALF].rearrange("p (q m u) -> p q m u", q=2, u=2),
                    in_=held[b][:].rearrange("p (q u m) -> p q m u", q=2, u=2),
                )
            return turned

        def weave(rows, vector_cols=HALF):
            woven = ring.tile([P, UNIT], BF16, name="woven", bufs=3, align_bytes=64)
            for copy, lo, hi in ((nc.vector.tensor_copy, 0, vector_cols), (nc.scalar.copy, vector_cols, HALF)):
                if lo < hi:
                    copy(
                        out=woven[:, PACK * lo:PACK * hi].rearrange("p (c i t) -> p c t i", i=RUN, t=PACK),
                        in_=rows.rearrange("p (t j) -> p t j", t=PACK)[:, :, lo:hi].rearrange(
                            "p t (c i) -> p c t i", i=RUN),
                    )
            return woven

        def quantise(key, unit):
            name, bufs = ("ctrl", 4) if key[0] == "ctrl" else ("%s_%d_%d" % key, 1)
            codes = keep.tile([P, HALF], U32, name="codes_" + name, bufs=bufs, align_bytes=64)
            scales = keep.tile([P, HALF], U8, name="scales_" + name, bufs=bufs, align_bytes=64)
            nc.vector.quantize_mx(out=codes[:].bitcast(FP8X4), scales=scales[:], in_=unit[:])
            mx[key] = (codes, scales)

        def matmul(acc, left, quarter, right, start, stop):
            cols = slice(quarter * P, (quarter + 1) * P)
            nc.tensor.matmul_mx(
                out=acc[:],
                lhsT=mx[left][0][:, cols].bitcast(FP8X4),
                lhsT_scale=mx[left][1][:, cols],
                rhs=mx[right][0][:].bitcast(FP8X4),
                rhs_scale=mx[right][1][:],
                start=start,
                stop=stop,
            )

        def coef_pass(acc, h, g, t, k):
            left, quarter = (("pinv", 0, k), t) if g == 0 else (("pinv", 1, t), k)
            matmul(acc, left, quarter, ("treat", h, k), k == 0, k == OBS_GROUPS - 1)

        def coef_tile(acc, h, g, t):
            for k in range(OBS_GROUPS):
                coef_pass(acc, h, g, t, k)
            return acc

        def shrink_out(acc, h, g, t):
            if t == 0:
                coef_rows[h, g] = ring.tile([P, UNIT], BF16, name="coef_rows")
            nc.scalar.activation(
                out=coef_rows[h, g][:, t * HALF:(t + 1) * HALF], in_=acc[:], func=COPY,
                scale=shrink_f32[:, g * PACK + t:g * PACK + t + 1],
            )

        def negate_sigma(lo, hi):
            nc.vector.tensor_scalar(
                out=neg_sigma[:, lo:hi], in0=sigma_bf[:].rearrange("p g t -> p (g t)")[:, lo:hi],
                scalar1=-1.0, scalar2=None, op0=MULT,
            )

        def prescale(g, t, engine):
            result[g, t] = ring.tile([P, N_TREAT], F32, name="result", bufs=RESULT_TILES)
            src = treat_raw[g][:].rearrange("p (h t j) -> p h t j", h=2, t=PACK)[:, :, t, :]
            dst = result[g, t][:].rearrange("p (h j) -> p h j", h=2)
            factor = neg_sigma[:, g * PACK + t:g * PACK + t + 1]
            if engine == "vector":
                nc.vector.tensor_scalar(out=dst, in0=src, scalar1=factor, scalar2=None, op0=MULT)
            elif engine == "gpsimd":
                nc.gpsimd.tensor_scalar(out=dst, in0=src, scalar1=factor, scalar2=0.0, op0=MULT, op1=ADD)
            else:
                nc.scalar.activation(out=dst, in_=src, func=COPY, scale=factor)

        def fit(g, t, h):
            acc = next_bank()
            for c in range(CTRL_GROUPS):
                matmul(acc, ("ctrl", g, t // 2), (t % 2) * 2 + c, ("coef", h, c), c == 0, c == CTRL_GROUPS - 1)
            return acc

        def finish(acc, g, t, h):
            part = result[g, t][:, h * HALF:(h + 1) * HALF]
            nc.vector.scalar_tensor_tensor(
                out=part, in0=acc[:], scalar=neg_sigma[:, g * PACK + t:g * PACK + t + 1], in1=part,
                op0=MULT, op1=SUBTRACT,
            )

        def store(g, t, lo, hi):
            rows = out[g * K_PASS:(g + 1) * K_PASS, :].rearrange("(p t) j -> p t j", t=PACK)
            nc.sync.dma_start(out=rows[:, t, lo:hi], in_=result[g, t][:, lo:hi])

        def turn_controls(g):
            held = [turn(tidy[g, pair], (next_bank(), next_bank()), True) for pair in range(2)]
            return [unload(two) for two in held]

        sums = [bank(2 + t) for t in range(PACK)]
        for s in range(2 * PACK):
            h, i = divmod(s, PACK)
            held = turn(pinv_raw[s], [bank(b) for b in ((0, 1), (6, 7))[s % 2]], False)
            if 0 < s <= PACK:
                for t in range(PACK):
                    coef_pass(sums[t], 0, 0, t, s - 1)
            elif s > PACK:
                acc = coef_tile(bank(2 + i - 1), 0, 1, i - 1)
            turned = unload(held)
            if h == 0:
                woven = weave(treat_unit(i, h), VECTOR_COLS_TREAT)
            else:
                shrink_out(sums[i], 0, 0, i)
                if i > 0:
                    shrink_out(acc, 0, 1, i - 1)
                woven = weave(treat_unit(i, h))
            quantise(("pinv", h, i), turned)
            quantise(("treat", h, i), woven)

        tidy = {}
        for pair in range(2):
            tidy[0, pair] = sort_words(nc.scalar.copy, ctrl_unit(0, pair))
        early = [next_bank() for t in range(2)]
        for k in range(OBS_GROUPS - 1):
            for t in range(2):
                coef_pass(early[t], 1, 0, t, k)
        shrink_out(coef_tile(bank(2 + PACK - 1), 0, 1, PACK - 1), 0, 1, PACK - 1)
        for t in range(2):
            coef_pass(early[t], 1, 0, t, OBS_GROUPS - 1)
            shrink_out(early[t], 1, 0, t)
        negate_sigma(0, PACK + 2)
        for g in range(CTRL_GROUPS):
            woven = weave(coef_rows[0, g][:])
            prescale(0, 2 * g, "vector")
            quantise(("coef", 0, g), woven)
            prescale(0, 2 * g + 1, "vector")
        for t in range(2, PACK):
            shrink_out(coef_tile(next_bank(), 1, 0, t), 1, 0, t)
        turned = turn_controls(0)
        woven = weave(coef_rows[1, 0][:])
        tidy[1, 0] = sort_words(nc.vector.tensor_copy, ctrl_unit(1, 0))
        quantise(("coef", 1, 0), woven)
        for pair in range(2):
            quantise(("ctrl", 0, pair), turned[pair])
        tidy[1, 1] = sort_words(nc.vector.tensor_copy, ctrl_unit(1, 1))
        prescale(1, 1, "vector")
        for t in range(PACK):
            shrink_out(coef_tile(next_bank(), 1, 1, t), 1, 1, t)
            if t == 0:
                prescale(1, 0, "scalar")

        sums = [fit(0, t, 0) for t in range(PACK)]
        woven = weave(coef_rows[1, 1][:], VECTOR_COLS_COEF)
        for t in range(PACK):
            finish(sums[t], 0, t, 0)
            store(0, t, 0, HALF)
            if t == 0:
                quantise(("coef", 1, 1), woven)
        for g in range(OBS_GROUPS):
            more = g + 1 < OBS_GROUPS
            if g > 0:
                for t in range(2):
                    for h in range(2):
                        finish(fit(g, t, h), g, t, h)
                    store(g, t, 0, N_TREAT)
            if more:
                turned = turn_controls(g + 1)
                quantise(("ctrl", g + 1, 0), turned[0])
            if g + 2 < OBS_GROUPS:
                for pair in range(2):
                    tidy[g + 2, pair] = sort_words(nc.scalar.copy, ctrl_unit(g + 2, pair))
            rest = [(t, 1) for t in range(PACK)] if g == 0 else [(t, h) for t in range(2, PACK) for h in range(2)]
            for i, (t, h) in enumerate(rest):
                finish(fit(g, t, h), g, t, h)
                if g == 0 or (not more and t == PACK - 1):
                    store(g, t, h * HALF, (h + 1) * HALF)
                elif h == 1:
                    store(g, t, 0, N_TREAT)
                if more and i == 0:
                    quantise(("ctrl", g + 1, 1), turned[1])
                    lo = PACK * (g + 1) + 2
                    hi = min(lo + PACK, OBS_GROUPS * PACK)
                    negate_sigma(lo, hi)
                    for r in range(lo, hi):
                        prescale(r // PACK, r % PACK, "gpsimd" if r < lo + GPSIMD_PRESCALES else "scalar")
